import numpy as np
import ml_dtypes


def mxq(x, axis, fmt="e4m3"):
    dtype, down = {"e4m3": (ml_dtypes.float8_e4m3fn, 7), "e5m2": (ml_dtypes.float8_e5m2, 14)}[fmt]
    v = np.moveaxis(np.asarray(x, np.float32).astype(ml_dtypes.bfloat16).astype(np.float64), axis, -1)
    blocks = v.reshape(v.shape[:-1] + (-1, 32))
    amax = np.abs(blocks).max(-1, keepdims=True)
    byte = np.maximum(np.where(amax > 0, np.frexp(amax)[1] - 1 + 127, 0) - down, 1)
    scale = np.exp2(byte - 127.0)
    codes = (blocks / scale).astype(np.float32).astype(dtype).astype(np.float64)
    return np.moveaxis((codes * scale).reshape(v.shape), -1, axis)


WIDE = False


def mx_kscale(k):
    if not WIDE:
        return np.ones(k)
    levels = np.array([10, -10, 5, -5, 0])
    if k % 512:
        return np.exp2(np.random.permutation(np.resize(levels, k // 32))).repeat(32)
    a = np.empty((k // 512, 16))
    for p in range(k // 512):
        a[p, :8] = np.random.permutation(np.resize(levels, 8))
        for g in range(8):
            far = levels[np.abs(levels - a[p, g]) >= 10]
            a[p, g + 8] = far[np.random.randint(len(far))]
    return np.exp2(a.ravel()).repeat(32)


def f64(x):
    return np.asarray(x).astype(np.float64)


def striped(idx):
    return np.tile(idx.reshape(-1, 16).T, (8, 1)).astype(np.uint16)


def unstriped(offs):
    return offs[:16].T.reshape(-1).astype(np.int64)


def pack_weight(w):
    k, n = w.shape
    w = f64(np.asarray(w, np.float32).astype(ml_dtypes.bfloat16)).reshape(k // 32, 32, n)
    amax = np.abs(w).max(1)
    byte = np.clip(np.where(amax > 0, np.frexp(amax)[1] - 1 + 127 - 7, 1), 1, 254)
    scaled = (w * np.exp2(127.0 - byte)[:, None, :]).reshape(k, n).astype(np.float32)
    words = np.ascontiguousarray(scaled.reshape(k // 512, 128, 4, n).transpose(0, 1, 3, 2)).astype(ml_dtypes.float8_e4m3fn).view(np.uint8)
    return words, np.ascontiguousarray(byte.astype(np.uint8).reshape(k // 512, 16, n))


def unpack_weight(words, scales):
    g, p, n, _ = words.shape
    vals = np.ascontiguousarray(words).view(ml_dtypes.float8_e4m3fn).astype(np.float64) * np.repeat(np.exp2(scales.astype(np.float64) - 127.0), 8, axis=1)[..., None]
    return vals.transpose(0, 1, 3, 2).reshape(g * 512, n)


K, T, S, N = 512, 2048, 512, 256


def setup_inputs():
    n = np.random.standard_normal
    s = mx_kscale(K)[:, None]
    packed_xT = pack_weight(n((K, T)) * s)
    return {
        "x_words": packed_xT[0],
        "x_scales": packed_xT[1],
        "w1": (n((K, N)) / np.sqrt(K) / s).astype(np.float32),
        "w2": (n((K, N)) / np.sqrt(K) / s).astype(np.float32),
        "inten": (np.random.uniform(0.2, 2.0, (N, S))).astype(np.float32),
        "offs": striped(np.random.permutation(T)[:S]),
        "up": striped(np.random.permutation(S)),
        "upb": striped(np.random.permutation(S)),
    }


def reference(x_words, x_scales, w1, w2, inten, offs, up, upb):
    xq = unpack_weight(x_words, x_scales)[:, unstriped(offs)]
    yk = mxq(f64(w1), 0, "e4m3").T @ xq
    tau = np.log(np.exp(yk) + 1.0)
    tra = np.exp(-1.0 * tau)
    ys = mxq(f64(w2), 0, "e4m3").T @ xq
    src = np.exp(0.5 * ys)
    ia = f64(inten)[:, unstriped(up)] * tra + src * (-1.0 * tra + 1.0)
    return ia[:, unstriped(upb)] * tra + src * (-1.0 * tra + 1.0)

@@ -1,0 +1,163 @@
+from contextlib import ExitStack
+
+import concourse.mybir as mybir
+
+K, T, S, N = 512, 2048, 512, 256
+FLOPS = 2 * 2 * K * N * S
+
+F32 = mybir.dt.float32
+BF16 = mybir.dt.bfloat16
+I32 = mybir.dt.int32
+U32 = mybir.dt.uint32
+U16 = mybir.dt.uint16
+U8 = mybir.dt.uint8
+FP8X4 = mybir.dt.float8_e4m3fn_x4
+ACT = mybir.ActivationFunctionType
+ALU = mybir.AluOpType
+
+P = 128
+PACK = 4
+BLOCKS = N // P
+HALF = S // 2
+LIST_COLS = S // 16
+
+
+def tile_picked_yrte_two_p_kernel(
+    tc, x_words, x_scales, w1, w2, inten, offs, up, upb, out
+):
+    nc = tc.nc
+    with ExitStack() as ctx:
+        keep = ctx.enter_context(tc.tile_pool(name="keep", bufs=1))
+        psum = ctx.enter_context(tc.psum_pool(name="psum", bufs=1))
+
+        offs_sb = keep.tile([P, LIST_COLS], U16, name="offs_sb")
+        up_sb = keep.tile([P, LIST_COLS], U16, name="up_sb")
+        upb_sb = keep.tile([P, LIST_COLS], U16, name="upb_sb")
+        table_words = keep.tile([P, T], U32, name="table_words", align_bytes=64)
+        table_scales = keep.tile([P, T], U8, name="table_scales", align_bytes=64)
+        warm = keep.tile([P, 1], F32, name="warm")
+        warm_out = keep.tile([P, 1], F32, name="warm_out")
+        inten_sb = [keep.tile([P, S], F32, name=f"inten_sb{b}") for b in range(BLOCKS)]
+        w_raw = [keep.tile([P, PACK, N], F32, name=f"w_raw{i}") for i in range(2)]
+
+        nc.vector.memset(table_scales[:].bitcast(I32), 0)
+        nc.vector.memset(warm[:], 0.0)
+        for q in range(4):
+            nc.scalar.dma_start(
+                table_scales[32 * q : 32 * q + 4, :].bitcast(I32),
+                x_scales[0, 4 * q : 4 * q + 4, :].bitcast(I32),
+            )
+        nc.scalar.activation(warm_out[:], warm[:], ACT.Exp)
+
+        nc.sync.dma_start(offs_sb[:], offs)
+        nc.sync.dma_start(up_sb[:], up)
+        nc.sync.dma_start(inten_sb[0][:], inten[0:P, :])
+        for i, w in enumerate((w1, w2)):
+            nc.sync.dma_start(w_raw[i][:], w.rearrange("(p j) m -> p j m", j=PACK))
+        nc.sync.dma_start(
+            table_words[:].bitcast(I32),
+            x_words[0].rearrange("p n t -> p (n t)").bitcast(I32),
+        )
+        nc.sync.dma_start(inten_sb[1][:], inten[P : 2 * P, :])
+        nc.sync.dma_start(upb_sb[:], upb)
+
+        def half(h):
+            return slice(h * HALF, (h + 1) * HALF)
+
+        def list_half(h):
+            return slice(h * LIST_COLS // 2, (h + 1) * LIST_COLS // 2)
+
+        picked_scales = keep.tile([P, S], U8, name="picked_scales", align_bytes=64)
+        nc.vector.tensor_copy(picked_scales[:], table_scales[:].indirect(offs_sb[:]))
+
+        upwind = [keep.tile([P, S], F32, name=f"upwind{b}") for b in range(BLOCKS)]
+
+        def fetch_upwind(b):
+            for h in range(2):
+                nc.vector.tensor_copy(upwind[b][:, half(h)], inten_sb[b][:].indirect(up_sb[:, list_half(h)]))
+
+        fetch_upwind(0)
+
+        w_words, w_scales = [], []
+        for i in range(2):
+            grouped = keep.tile([P, N, PACK], BF16, name=f"grouped{i}", align_bytes=64)
+            nc.scalar.copy(
+                grouped[:].rearrange("p (c e) j -> p c j e", e=4),
+                w_raw[i][:].rearrange("p j (c e) -> p c j e", e=4),
+            )
+            words = keep.tile([P, N], U32, name=f"w_words{i}", align_bytes=64)
+            scales = keep.tile([P, N], U8, name=f"w_scales{i}", align_bytes=64)
+            nc.vector.quantize_mx(
+                out=words[:].bitcast(FP8X4), scales=scales[:], in_=grouped[:].rearrange("p m j -> p (m j)")
+            )
+            w_words.append(words)
+            w_scales.append(scales)
+
+        picked_words = keep.tile([P, S], U32, name="picked_words", align_bytes=64)
+        nc.vector.tensor_copy(picked_words[:], table_words[:].indirect(offs_sb[:]))
+
+        th, src, quarter = [], [], []
+        for b in range(BLOCKS):
+            cols = slice(b * P, (b + 1) * P)
+            banks = []
+            for i in range(2):
+                bank = psum.tile([P, S], F32, name=f"bank{b}{i}")
+                nc.tensor.matmul_mx(
+                    out=bank[:],
+                    lhsT=w_words[i][:, cols].bitcast(FP8X4),
+                    lhsT_scale=w_scales[i][:, cols],
+                    rhs=picked_words[:].bitcast(FP8X4),
+                    rhs_scale=picked_scales[:],
+                    start=True,
+                    stop=True,
+                )
+                banks.append(bank)
+            th.append(keep.tile([P, S], F32, name=f"th{b}"))
+            nc.scalar.activation(th[b][:], banks[0][:], ACT.Tanh, scale=-0.5)
+            src.append(keep.tile([P, S], F32, name=f"src{b}"))
+            nc.scalar.activation(src[b][:], banks[1][:], ACT.Exp, scale=0.5)
+        fetch_upwind(1)
+        for b in range(BLOCKS):
+            quarter.append(keep.tile([P, S], F32, name=f"quarter{b}"))
+            nc.scalar.activation(quarter[b][:], th[b][:], ACT.Copy, scale=0.25, bias=0.25)
+
+        through = [keep.tile([P, S], F32, name=f"through{b}") for b in range(BLOCKS)]
+        emitted = [keep.tile([P, S], F32, name=f"emitted{b}") for b in range(BLOCKS)]
+        first = [keep.tile([P, S], F32, name=f"first{b}") for b in range(BLOCKS)]
+        second = [keep.tile([P, S], F32, name=f"second{b}") for b in range(BLOCKS)]
+        result = [[keep.tile([P, HALF], F32, name=f"result{b}{h}") for h in range(2)] for b in range(BLOCKS)]
+
+        def step_through(b):
+            nc.vector.scalar_tensor_tensor(through[b][:], th[b][:], 1.0, upwind[b][:], ALU.add, ALU.mult)
+
+        def step_emitted(b):
+            nc.vector.scalar_tensor_tensor(emitted[b][:], th[b][:], -1.0, src[b][:], ALU.add, ALU.mult)
+
+        def step_first(b):
+            nc.vector.tensor_tensor(first[b][:], through[b][:], emitted[b][:], ALU.subtract)
+
+        def step_second(b, h):
+            nc.vector.tensor_tensor(
+                second[b][:, half(h)], first[b][:].indirect(upb_sb[:, list_half(h)]), quarter[b][:, half(h)], ALU.mult
+            )
+
+        def step_result(b, h):
+            nc.vector.scalar_tensor_tensor(
+                result[b][h][:], emitted[b][:, half(h)], -0.5, second[b][:, half(h)], ALU.mult, ALU.add
+            )
+            nc.sync.dma_start(out[b * P : (b + 1) * P, half(h)], result[b][h][:])
+
+        step_through(0)
+        step_emitted(0)
+        step_through(1)
+        step_first(0)
+        step_emitted(1)
+        step_second(0, 0)
+        step_first(1)
+        step_second(0, 1)
+        step_result(0, 0)
+        step_second(1, 0)
+        step_result(0, 1)
+        step_second(1, 1)
+        step_result(1, 0)
+        step_result(1, 1)

@@ -20,6 +20,8 @@ PACK = 4
 BLOCKS = N // P
 HALF = S // 2
 LIST_COLS = S // 16
+WIDE = 704
+SPARE = 16
 
 
 def tile_picked_yrte_two_p_kernel(
@@ -37,28 +39,34 @@ def tile_picked_yrte_two_p_kernel(
         table_scales = keep.tile([P, T], U8, name="table_scales", align_bytes=64)
         warm = keep.tile([P, 1], F32, name="warm")
         warm_out = keep.tile([P, 1], F32, name="warm_out")
-        inten_sb = [keep.tile([P, S], F32, name=f"inten_sb{b}") for b in range(BLOCKS)]
+        inten_sb = keep.tile([P, BLOCKS * S], F32, name="inten_sb")
         w_raw = [keep.tile([P, PACK, N], F32, name=f"w_raw{i}") for i in range(2)]
 
         nc.vector.memset(table_scales[:].bitcast(I32), 0)
         nc.vector.memset(warm[:], 0.0)
-        for q in range(4):
-            nc.scalar.dma_start(
+
+        def load_scale_rows(queue, q):
+            queue.dma_start(
                 table_scales[32 * q : 32 * q + 4, :].bitcast(I32),
                 x_scales[0, 4 * q : 4 * q + 4, :].bitcast(I32),
             )
+
+        nc.scalar.dma_start(inten_sb[:, S:], inten[0:P, :])
+        for q in range(2):
+            load_scale_rows(nc.scalar, q)
         nc.scalar.activation(warm_out[:], warm[:], ACT.Exp)
 
         nc.sync.dma_start(offs_sb[:], offs)
         nc.sync.dma_start(up_sb[:], up)
-        nc.sync.dma_start(inten_sb[0][:], inten[0:P, :])
         for i, w in enumerate((w1, w2)):
             nc.sync.dma_start(w_raw[i][:], w.rearrange("(p j) m -> p j m", j=PACK))
+        for q in range(2, 4):
+            load_scale_rows(nc.sync, q)
         nc.sync.dma_start(
             table_words[:].bitcast(I32),
             x_words[0].rearrange("p n t -> p (n t)").bitcast(I32),
         )
-        nc.sync.dma_start(inten_sb[1][:], inten[P : 2 * P, :])
+        nc.sync.dma_start(inten_sb[:, :S], inten[P : 2 * P, :])
         nc.sync.dma_start(upb_sb[:], upb)
 
         def half(h):
@@ -72,11 +80,8 @@ def tile_picked_yrte_two_p_kernel(
 
         upwind = [keep.tile([P, S], F32, name=f"upwind{b}") for b in range(BLOCKS)]
 
-        def fetch_upwind(b):
-            for h in range(2):
-                nc.vector.tensor_copy(upwind[b][:, half(h)], inten_sb[b][:].indirect(up_sb[:, list_half(h)]))
-
-        fetch_upwind(0)
+        for h in range(2):
+            nc.vector.tensor_copy(upwind[0][:, half(h)], inten_sb[:, S:].indirect(up_sb[:, list_half(h)]))
 
         w_words, w_scales = [], []
         for i in range(2):
@@ -94,38 +99,39 @@ def tile_picked_yrte_two_p_kernel(
             w_scales.append(scales)
 
         picked_words = keep.tile([P, S], U32, name="picked_words", align_bytes=64)
-        nc.vector.tensor_copy(picked_words[:], table_words[:].indirect(offs_sb[:]))
+        th = [keep.tile([P, S], F32, name=f"th{b}") for b in range(BLOCKS)]
+        src = [keep.tile([P, S], F32, name=f"src{b}") for b in range(BLOCKS)]
+        quarter = []
 
-        th, src, quarter = [], [], []
-        for b in range(BLOCKS):
-            cols = slice(b * P, (b + 1) * P)
-            banks = []
-            for i in range(2):
-                bank = psum.tile([P, S], F32, name=f"bank{b}{i}")
+        def products(b, cols):
+            rows = slice(b * P, (b + 1) * P)
+            for i, (dst, func, scale) in enumerate(((th[b], ACT.Tanh, -0.5), (src[b], ACT.Exp, 0.5))):
+                bank = psum.tile([P, cols.stop - cols.start], F32, name=f"bank{b}{i}_{cols.start}")
                 nc.tensor.matmul_mx(
                     out=bank[:],
-                    lhsT=w_words[i][:, cols].bitcast(FP8X4),
-                    lhsT_scale=w_scales[i][:, cols],
-                    rhs=picked_words[:].bitcast(FP8X4),
-                    rhs_scale=picked_scales[:],
+                    lhsT=w_words[i][:, rows].bitcast(FP8X4),
+                    lhsT_scale=w_scales[i][:, rows],
+                    rhs=picked_words[:, cols].bitcast(FP8X4),
+                    rhs_scale=picked_scales[:, cols],
                     start=True,
                     stop=True,
                 )
-                banks.append(bank)
-            th.append(keep.tile([P, S], F32, name=f"th{b}"))
-            nc.scalar.activation(th[b][:], banks[0][:], ACT.Tanh, scale=-0.5)
-            src.append(keep.tile([P, S], F32, name=f"src{b}"))
-            nc.scalar.activation(src[b][:], banks[1][:], ACT.Exp, scale=0.5)
-        fetch_upwind(1)
+                nc.scalar.activation(dst[:, cols], bank[:], func, scale=scale)
+
+        for h in range(2):
+            nc.vector.tensor_copy(picked_words[:, half(h)], table_words[:].indirect(offs_sb[:, list_half(h)]))
+            products(0, half(h))
+        products(1, slice(0, S))
+        nc.vector.tensor_copy(upwind[1][:], inten_sb[:, :WIDE].indirect(up_sb[:]))
         for b in range(BLOCKS):
             quarter.append(keep.tile([P, S], F32, name=f"quarter{b}"))
             nc.scalar.activation(quarter[b][:], th[b][:], ACT.Copy, scale=0.25, bias=0.25)
 
         through = [keep.tile([P, S], F32, name=f"through{b}") for b in range(BLOCKS)]
         emitted = [keep.tile([P, S], F32, name=f"emitted{b}") for b in range(BLOCKS)]
-        first = [keep.tile([P, S], F32, name=f"first{b}") for b in range(BLOCKS)]
+        first = [keep.tile([P, S + SPARE], F32, name="first0"), keep.tile([P, S], F32, name="first1")]
+        nc.gpsimd.memset(first[0][:, S:], 0.0)
         second = [keep.tile([P, S], F32, name=f"second{b}") for b in range(BLOCKS)]
-        result = [[keep.tile([P, HALF], F32, name=f"result{b}{h}") for h in range(2)] for b in range(BLOCKS)]
 
         def step_through(b):
             nc.vector.scalar_tensor_tensor(through[b][:], th[b][:], 1.0, upwind[b][:], ALU.add, ALU.mult)
@@ -134,30 +140,29 @@ def tile_picked_yrte_two_p_kernel(
             nc.vector.scalar_tensor_tensor(emitted[b][:], th[b][:], -1.0, src[b][:], ALU.add, ALU.mult)
 
         def step_first(b):
-            nc.vector.tensor_tensor(first[b][:], through[b][:], emitted[b][:], ALU.subtract)
+            nc.vector.tensor_tensor(first[b][:, :S], through[b][:], emitted[b][:], ALU.subtract)
 
-        def step_second(b, h):
-            nc.vector.tensor_tensor(
-                second[b][:, half(h)], first[b][:].indirect(upb_sb[:, list_half(h)]), quarter[b][:, half(h)], ALU.mult
-            )
+        def step_second(b, cols):
+            offsets = upb_sb[:, cols.start // 16 : cols.stop // 16]
+            nc.vector.tensor_tensor(second[b][:, cols], first[b][:].indirect(offsets), quarter[b][:, cols], ALU.mult)
 
-        def step_result(b, h):
+        def step_result(b, cols, queue):
+            result = keep.tile([P, cols.stop - cols.start], F32, name=f"result{b}_{cols.start}")
             nc.vector.scalar_tensor_tensor(
-                result[b][h][:], emitted[b][:, half(h)], -0.5, second[b][:, half(h)], ALU.mult, ALU.add
+                result[:], emitted[b][:, cols], -0.5, second[b][:, cols], ALU.mult, ALU.add
             )
-            nc.sync.dma_start(out[b * P : (b + 1) * P, half(h)], result[b][h][:])
+            queue.dma_start(out[b * P : (b + 1) * P, cols], result[:])
 
+        whole = slice(0, S)
         step_through(0)
         step_emitted(0)
         step_through(1)
         step_first(0)
         step_emitted(1)
-        step_second(0, 0)
+        step_second(0, whole)
         step_first(1)
-        step_second(0, 1)
-        step_result(0, 0)
-        step_second(1, 0)
-        step_result(0, 1)
-        step_second(1, 1)
-        step_result(1, 0)
-        step_result(1, 1)
+        step_result(0, whole, nc.sync)
+        step_second(1, half(0))
+        step_second(1, half(1))
+        step_result(1, half(0), nc.sync)
+        step_result(1, half(1), nc.scalar)

@@ -36,32 +36,24 @@ def tile_picked_yrte_two_p_kernel(
         up_sb = keep.tile([P, LIST_COLS], U16, name="up_sb")
         upb_sb = keep.tile([P, LIST_COLS], U16, name="upb_sb")
         table_words = keep.tile([P, T], U32, name="table_words", align_bytes=64)
-        table_scales = keep.tile([P, T], U8, name="table_scales", align_bytes=64)
+        table_scales = keep.tile([P, T], U8, name="table_scales", tag="scales_then_upwind", align_bytes=64)
         warm = keep.tile([P, 1], F32, name="warm")
         warm_out = keep.tile([P, 1], F32, name="warm_out")
         inten_sb = keep.tile([P, BLOCKS * S], F32, name="inten_sb")
         w_raw = [keep.tile([P, PACK, N], F32, name=f"w_raw{i}") for i in range(2)]
 
+        plane = keep.tile([P, S], U8, name="plane", align_bytes=64)
         nc.vector.memset(table_scales[:].bitcast(I32), 0)
         nc.vector.memset(warm[:], 0.0)
-
-        def load_scale_rows(queue, q):
-            queue.dma_start(
-                table_scales[32 * q : 32 * q + 4, :].bitcast(I32),
-                x_scales[0, 4 * q : 4 * q + 4, :].bitcast(I32),
-            )
-
-        nc.scalar.dma_start(inten_sb[:, S:], inten[0:P, :])
-        for q in range(2):
-            load_scale_rows(nc.scalar, q)
+        nc.vector.memset(plane[:].bitcast(I32), 0)
         nc.scalar.activation(warm_out[:], warm[:], ACT.Exp)
 
         nc.sync.dma_start(offs_sb[:], offs)
         nc.sync.dma_start(up_sb[:], up)
+        nc.sync.dma_start(table_scales[0:P:8, :].bitcast(I32), x_scales[0].bitcast(I32))
+        nc.sync.dma_start(inten_sb[:, S:], inten[0:P, :])
         for i, w in enumerate((w1, w2)):
             nc.sync.dma_start(w_raw[i][:], w.rearrange("(p j) m -> p j m", j=PACK))
-        for q in range(2, 4):
-            load_scale_rows(nc.sync, q)
         nc.sync.dma_start(
             table_words[:].bitcast(I32),
             x_words[0].rearrange("p n t -> p (n t)").bitcast(I32),
@@ -77,8 +69,13 @@ def tile_picked_yrte_two_p_kernel(
 
         picked_scales = keep.tile([P, S], U8, name="picked_scales", align_bytes=64)
         nc.vector.tensor_copy(picked_scales[:], table_scales[:].indirect(offs_sb[:]))
+        for r in range(4):
+            nc.scalar.dma_start(plane[r:P:32, :].bitcast(I32), picked_scales[8 * r : P : 32, :].bitcast(I32))
 
-        upwind = [keep.tile([P, S], F32, name=f"upwind{b}") for b in range(BLOCKS)]
+        upwind = [
+            keep.tile([P, S], F32, name="upwind0", tag="scales_then_upwind", align_bytes=64),
+            keep.tile([P, S], F32, name="upwind1"),
+        ]
 
         for h in range(2):
             nc.vector.tensor_copy(upwind[0][:, half(h)], inten_sb[:, S:].indirect(up_sb[:, list_half(h)]))
@@ -112,7 +109,7 @@ def tile_picked_yrte_two_p_kernel(
                     lhsT=w_words[i][:, rows].bitcast(FP8X4),
                     lhsT_scale=w_scales[i][:, rows],
                     rhs=picked_words[:, cols].bitcast(FP8X4),
-                    rhs_scale=picked_scales[:, cols],
+                    rhs_scale=plane[:, cols],
                     start=True,
                     stop=True,
                 )

@@ -17,9 +17,13 @@ ALU = mybir.AluOpType
 
 P = 128
 PACK = 4
+QUADRANT = 32
+ROWS_PER_QUADRANT = 4
+SPREAD = P // (K // 32)
+LINE = 4
+GROUP = 16
 BLOCKS = N // P
 HALF = S // 2
-LIST_COLS = S // 16
 WIDE = 704
 SPARE = 16
 
@@ -28,64 +32,69 @@ def tile_picked_yrte_two_p_kernel(
     tc, x_words, x_scales, w1, w2, inten, offs, up, upb, out
 ):
     nc = tc.nc
+    whole = slice(0, S)
+    halves = [slice(h * HALF, (h + 1) * HALF) for h in range(2)]
+
+    def entries(list_tile, cols):
+        return list_tile[:, cols.start // GROUP : cols.stop // GROUP]
+
+    def rows(b):
+        return slice(b * P, (b + 1) * P)
+
     with ExitStack() as ctx:
         keep = ctx.enter_context(tc.tile_pool(name="keep", bufs=1))
         psum = ctx.enter_context(tc.psum_pool(name="psum", bufs=1))
 
-        offs_sb = keep.tile([P, LIST_COLS], U16, name="offs_sb")
-        up_sb = keep.tile([P, LIST_COLS], U16, name="up_sb")
-        upb_sb = keep.tile([P, LIST_COLS], U16, name="upb_sb")
+        offs_sb = keep.tile([P, S // GROUP], U16, name="offs_sb")
+        up_sb = keep.tile([P, S // GROUP], U16, name="up_sb")
+        upb_sb = keep.tile([P, S // GROUP], U16, name="upb_sb")
         table_words = keep.tile([P, T], U32, name="table_words", align_bytes=64)
         table_scales = keep.tile([P, T], U8, name="table_scales", tag="scales_then_upwind", align_bytes=64)
-        warm = keep.tile([P, 1], F32, name="warm")
-        warm_out = keep.tile([P, 1], F32, name="warm_out")
+        zeros = keep.tile([P, SPARE], F32, name="zeros")
         inten_sb = keep.tile([P, BLOCKS * S], F32, name="inten_sb")
         w_raw = [keep.tile([P, PACK, N], F32, name=f"w_raw{i}") for i in range(2)]
+        scale_plane = keep.tile([P, S], U8, name="scale_plane", align_bytes=64)
+        first = [keep.tile([P, S + SPARE], F32, name="first0"), keep.tile([P, S], F32, name="first1")]
 
-        plane = keep.tile([P, S], U8, name="plane", align_bytes=64)
         nc.vector.memset(table_scales[:].bitcast(I32), 0)
-        nc.vector.memset(warm[:], 0.0)
-        nc.vector.memset(plane[:].bitcast(I32), 0)
-        nc.scalar.activation(warm_out[:], warm[:], ACT.Exp)
+        nc.vector.memset(zeros[:], 0.0)
+        nc.vector.memset(scale_plane[:].bitcast(I32), 0)
+        nc.scalar.activation(first[0][:, S:], zeros[:], ACT.Exp)
 
         nc.sync.dma_start(offs_sb[:], offs)
         nc.sync.dma_start(up_sb[:], up)
-        nc.sync.dma_start(table_scales[0:P:8, :].bitcast(I32), x_scales[0].bitcast(I32))
-        nc.sync.dma_start(inten_sb[:, S:], inten[0:P, :])
-        for i, w in enumerate((w1, w2)):
-            nc.sync.dma_start(w_raw[i][:], w.rearrange("(p j) m -> p j m", j=PACK))
+        nc.sync.dma_start(table_scales[0:P:SPREAD, :].bitcast(I32), x_scales[0].bitcast(I32))
+        nc.sync.dma_start(inten_sb[:, S:], inten[rows(0), :])
+        for raw, w in zip(w_raw, (w1, w2)):
+            nc.sync.dma_start(raw[:], w.rearrange("(p j) m -> p j m", j=PACK))
         nc.sync.dma_start(
             table_words[:].bitcast(I32),
             x_words[0].rearrange("p n t -> p (n t)").bitcast(I32),
         )
-        nc.sync.dma_start(inten_sb[:, :S], inten[P : 2 * P, :])
+        nc.sync.dma_start(inten_sb[:, :S], inten[rows(1), :])
         nc.sync.dma_start(upb_sb[:], upb)
-
-        def half(h):
-            return slice(h * HALF, (h + 1) * HALF)
-
-        def list_half(h):
-            return slice(h * LIST_COLS // 2, (h + 1) * LIST_COLS // 2)
 
         picked_scales = keep.tile([P, S], U8, name="picked_scales", align_bytes=64)
         nc.vector.tensor_copy(picked_scales[:], table_scales[:].indirect(offs_sb[:]))
-        for r in range(4):
-            nc.scalar.dma_start(plane[r:P:32, :].bitcast(I32), picked_scales[8 * r : P : 32, :].bitcast(I32))
+        for r in range(ROWS_PER_QUADRANT):
+            nc.scalar.dma_start(
+                scale_plane[r:P:QUADRANT, :].bitcast(I32),
+                picked_scales[SPREAD * r : P : QUADRANT, :].bitcast(I32),
+            )
 
         upwind = [
             keep.tile([P, S], F32, name="upwind0", tag="scales_then_upwind", align_bytes=64),
             keep.tile([P, S], F32, name="upwind1"),
         ]
-
-        for h in range(2):
-            nc.vector.tensor_copy(upwind[0][:, half(h)], inten_sb[:, S:].indirect(up_sb[:, list_half(h)]))
+        for cols in halves:
+            nc.vector.tensor_copy(upwind[0][:, cols], inten_sb[:, S:].indirect(entries(up_sb, cols)))
 
         w_words, w_scales = [], []
-        for i in range(2):
+        for i, interleave in enumerate((nc.vector.tensor_copy, nc.scalar.copy)):
             grouped = keep.tile([P, N, PACK], BF16, name=f"grouped{i}", align_bytes=64)
-            nc.scalar.copy(
-                grouped[:].rearrange("p (c e) j -> p c j e", e=4),
-                w_raw[i][:].rearrange("p j (c e) -> p c j e", e=4),
+            interleave(
+                grouped[:].rearrange("p (c e) j -> p c j e", e=LINE),
+                w_raw[i][:].rearrange("p j (c e) -> p c j e", e=LINE),
             )
             words = keep.tile([P, N], U32, name=f"w_words{i}", align_bytes=64)
             scales = keep.tile([P, N], U8, name=f"w_scales{i}", align_bytes=64)
@@ -98,36 +107,33 @@ def tile_picked_yrte_two_p_kernel(
         picked_words = keep.tile([P, S], U32, name="picked_words", align_bytes=64)
         th = [keep.tile([P, S], F32, name=f"th{b}") for b in range(BLOCKS)]
         src = [keep.tile([P, S], F32, name=f"src{b}") for b in range(BLOCKS)]
-        quarter = []
 
         def products(b, cols):
-            rows = slice(b * P, (b + 1) * P)
             for i, (dst, func, scale) in enumerate(((th[b], ACT.Tanh, -0.5), (src[b], ACT.Exp, 0.5))):
                 bank = psum.tile([P, cols.stop - cols.start], F32, name=f"bank{b}{i}_{cols.start}")
                 nc.tensor.matmul_mx(
                     out=bank[:],
-                    lhsT=w_words[i][:, rows].bitcast(FP8X4),
-                    lhsT_scale=w_scales[i][:, rows],
+                    lhsT=w_words[i][:, rows(b)].bitcast(FP8X4),
+                    lhsT_scale=w_scales[i][:, rows(b)],
                     rhs=picked_words[:, cols].bitcast(FP8X4),
-                    rhs_scale=plane[:, cols],
+                    rhs_scale=scale_plane[:, cols],
                     start=True,
                     stop=True,
                 )
                 nc.scalar.activation(dst[:, cols], bank[:], func, scale=scale)
 
-        for h in range(2):
-            nc.vector.tensor_copy(picked_words[:, half(h)], table_words[:].indirect(offs_sb[:, list_half(h)]))
-            products(0, half(h))
-        products(1, slice(0, S))
+        for cols in halves:
+            nc.vector.tensor_copy(picked_words[:, cols], table_words[:].indirect(entries(offs_sb, cols)))
+            products(0, cols)
+        products(1, whole)
         nc.vector.tensor_copy(upwind[1][:], inten_sb[:, :WIDE].indirect(up_sb[:]))
+
+        quarter = [keep.tile([P, S], F32, name=f"quarter{b}") for b in range(BLOCKS)]
         for b in range(BLOCKS):
-            quarter.append(keep.tile([P, S], F32, name=f"quarter{b}"))
             nc.scalar.activation(quarter[b][:], th[b][:], ACT.Copy, scale=0.25, bias=0.25)
 
         through = [keep.tile([P, S], F32, name=f"through{b}") for b in range(BLOCKS)]
         emitted = [keep.tile([P, S], F32, name=f"emitted{b}") for b in range(BLOCKS)]
-        first = [keep.tile([P, S + SPARE], F32, name="first0"), keep.tile([P, S], F32, name="first1")]
-        nc.gpsimd.memset(first[0][:, S:], 0.0)
         second = [keep.tile([P, S], F32, name=f"second{b}") for b in range(BLOCKS)]
 
         def step_through(b):
@@ -140,17 +146,17 @@ def tile_picked_yrte_two_p_kernel(
             nc.vector.tensor_tensor(first[b][:, :S], through[b][:], emitted[b][:], ALU.subtract)
 
         def step_second(b, cols):
-            offsets = upb_sb[:, cols.start // 16 : cols.stop // 16]
-            nc.vector.tensor_tensor(second[b][:, cols], first[b][:].indirect(offsets), quarter[b][:, cols], ALU.mult)
+            nc.vector.tensor_tensor(
+                second[b][:, cols], first[b][:].indirect(entries(upb_sb, cols)), quarter[b][:, cols], ALU.mult
+            )
 
         def step_result(b, cols, queue):
             result = keep.tile([P, cols.stop - cols.start], F32, name=f"result{b}_{cols.start}")
             nc.vector.scalar_tensor_tensor(
                 result[:], emitted[b][:, cols], -0.5, second[b][:, cols], ALU.mult, ALU.add
             )
-            queue.dma_start(out[b * P : (b + 1) * P, cols], result[:])
+            queue.dma_start(out[rows(b), cols], result[:])
 
-        whole = slice(0, S)
         step_through(0)
         step_emitted(0)
         step_through(1)
@@ -159,7 +165,7 @@ def tile_picked_yrte_two_p_kernel(
         step_second(0, whole)
         step_first(1)
         step_result(0, whole, nc.sync)
-        step_second(1, half(0))
-        step_second(1, half(1))
-        step_result(1, half(0), nc.sync)
-        step_result(1, half(1), nc.scalar)
+        for cols in halves:
+            step_second(1, cols)
+        for cols, queue in zip(halves, (nc.sync, nc.scalar)):
+            step_result(1, cols, queue)

from contextlib import ExitStack

import concourse.mybir as mybir

K, T, S, N = 512, 2048, 512, 256
FLOPS = 2 * 2 * K * N * S

F32 = mybir.dt.float32
BF16 = mybir.dt.bfloat16
I32 = mybir.dt.int32
U32 = mybir.dt.uint32
U16 = mybir.dt.uint16
U8 = mybir.dt.uint8
FP8X4 = mybir.dt.float8_e4m3fn_x4
ACT = mybir.ActivationFunctionType
ALU = mybir.AluOpType

P = 128
PACK = 4
QUADRANT = 32
ROWS_PER_QUADRANT = 4
SPREAD = P // (K // 32)
LINE = 4
GROUP = 16
BLOCKS = N // P
HALF = S // 2
WIDE = 704
SPARE = 16


def tile_picked_yrte_two_p_kernel(
    tc, x_words, x_scales, w1, w2, inten, offs, up, upb, out
):
    nc = tc.nc
    whole = slice(0, S)
    halves = [slice(h * HALF, (h + 1) * HALF) for h in range(2)]

    def entries(list_tile, cols):
        return list_tile[:, cols.start // GROUP : cols.stop // GROUP]

    def rows(b):
        return slice(b * P, (b + 1) * P)

    with ExitStack() as ctx:
        keep = ctx.enter_context(tc.tile_pool(name="keep", bufs=1))
        psum = ctx.enter_context(tc.psum_pool(name="psum", bufs=1))

        offs_sb = keep.tile([P, S // GROUP], U16, name="offs_sb")
        up_sb = keep.tile([P, S // GROUP], U16, name="up_sb")
        upb_sb = keep.tile([P, S // GROUP], U16, name="upb_sb")
        table_words = keep.tile([P, T], U32, name="table_words", align_bytes=64)
        table_scales = keep.tile([P, T], U8, name="table_scales", tag="scales_then_upwind", align_bytes=64)
        zeros = keep.tile([P, SPARE], F32, name="zeros")
        inten_sb = keep.tile([P, BLOCKS * S], F32, name="inten_sb")
        w_raw = [keep.tile([P, PACK, N], F32, name=f"w_raw{i}") for i in range(2)]
        scale_plane = keep.tile([P, S], U8, name="scale_plane", align_bytes=64)
        first = [keep.tile([P, S + SPARE], F32, name="first0"), keep.tile([P, S], F32, name="first1")]

        nc.vector.memset(table_scales[:].bitcast(I32), 0)
        nc.vector.memset(zeros[:], 0.0)
        nc.vector.memset(scale_plane[:].bitcast(I32), 0)
        nc.scalar.activation(first[0][:, S:], zeros[:], ACT.Exp)

        nc.sync.dma_start(offs_sb[:], offs)
        nc.sync.dma_start(up_sb[:], up)
        nc.sync.dma_start(table_scales[0:P:SPREAD, :].bitcast(I32), x_scales[0].bitcast(I32))
        nc.sync.dma_start(inten_sb[:, S:], inten[rows(0), :])
        for raw, w in zip(w_raw, (w1, w2)):
            nc.sync.dma_start(raw[:], w.rearrange("(p j) m -> p j m", j=PACK))
        nc.sync.dma_start(
            table_words[:].bitcast(I32),
            x_words[0].rearrange("p n t -> p (n t)").bitcast(I32),
        )
        nc.sync.dma_start(inten_sb[:, :S], inten[rows(1), :])
        nc.sync.dma_start(upb_sb[:], upb)

        picked_scales = keep.tile([P, S], U8, name="picked_scales", align_bytes=64)
        nc.vector.tensor_copy(picked_scales[:], table_scales[:].indirect(offs_sb[:]))
        for r in range(ROWS_PER_QUADRANT):
            nc.scalar.dma_start(
                scale_plane[r:P:QUADRANT, :].bitcast(I32),
                picked_scales[SPREAD * r : P : QUADRANT, :].bitcast(I32),
            )

        upwind = [
            keep.tile([P, S], F32, name="upwind0", tag="scales_then_upwind", align_bytes=64),
            keep.tile([P, S], F32, name="upwind1"),
        ]
        for cols in halves:
            nc.vector.tensor_copy(upwind[0][:, cols], inten_sb[:, S:].indirect(entries(up_sb, cols)))

        w_words, w_scales = [], []
        for i, interleave in enumerate((nc.vector.tensor_copy, nc.scalar.copy)):
            grouped = keep.tile([P, N, PACK], BF16, name=f"grouped{i}", align_bytes=64)
            interleave(
                grouped[:].rearrange("p (c e) j -> p c j e", e=LINE),
                w_raw[i][:].rearrange("p j (c e) -> p c j e", e=LINE),
            )
            words = keep.tile([P, N], U32, name=f"w_words{i}", align_bytes=64)
            scales = keep.tile([P, N], U8, name=f"w_scales{i}", align_bytes=64)
            nc.vector.quantize_mx(
                out=words[:].bitcast(FP8X4), scales=scales[:], in_=grouped[:].rearrange("p m j -> p (m j)")
            )
            w_words.append(words)
            w_scales.append(scales)

        picked_words = keep.tile([P, S], U32, name="picked_words", align_bytes=64)
        th = [keep.tile([P, S], F32, name=f"th{b}") for b in range(BLOCKS)]
        src = [keep.tile([P, S], F32, name=f"src{b}") for b in range(BLOCKS)]

        def products(b, cols):
            for i, (dst, func, scale) in enumerate(((th[b], ACT.Tanh, -0.5), (src[b], ACT.Exp, 0.5))):
                bank = psum.tile([P, cols.stop - cols.start], F32, name=f"bank{b}{i}_{cols.start}")
                nc.tensor.matmul_mx(
                    out=bank[:],
                    lhsT=w_words[i][:, rows(b)].bitcast(FP8X4),
                    lhsT_scale=w_scales[i][:, rows(b)],
                    rhs=picked_words[:, cols].bitcast(FP8X4),
                    rhs_scale=scale_plane[:, cols],
                    start=True,
                    stop=True,
                )
                nc.scalar.activation(dst[:, cols], bank[:], func, scale=scale)

        for cols in halves:
            nc.vector.tensor_copy(picked_words[:, cols], table_words[:].indirect(entries(offs_sb, cols)))
            products(0, cols)
        products(1, whole)
        nc.vector.tensor_copy(upwind[1][:], inten_sb[:, :WIDE].indirect(up_sb[:]))

        quarter = [keep.tile([P, S], F32, name=f"quarter{b}") for b in range(BLOCKS)]
        for b in range(BLOCKS):
            nc.scalar.activation(quarter[b][:], th[b][:], ACT.Copy, scale=0.25, bias=0.25)

        through = [keep.tile([P, S], F32, name=f"through{b}") for b in range(BLOCKS)]
        emitted = [keep.tile([P, S], F32, name=f"emitted{b}") for b in range(BLOCKS)]
        second = [keep.tile([P, S], F32, name=f"second{b}") for b in range(BLOCKS)]

        def step_through(b):
            nc.vector.scalar_tensor_tensor(through[b][:], th[b][:], 1.0, upwind[b][:], ALU.add, ALU.mult)

        def step_emitted(b):
            nc.vector.scalar_tensor_tensor(emitted[b][:], th[b][:], -1.0, src[b][:], ALU.add, ALU.mult)

        def step_first(b):
            nc.vector.tensor_tensor(first[b][:, :S], through[b][:], emitted[b][:], ALU.subtract)

        def step_second(b, cols):
            nc.vector.tensor_tensor(
                second[b][:, cols], first[b][:].indirect(entries(upb_sb, cols)), quarter[b][:, cols], ALU.mult
            )

        def step_result(b, cols, queue):
            result = keep.tile([P, cols.stop - cols.start], F32, name=f"result{b}_{cols.start}")
            nc.vector.scalar_tensor_tensor(
                result[:], emitted[b][:, cols], -0.5, second[b][:, cols], ALU.mult, ALU.add
            )
            queue.dma_start(out[rows(b), cols], result[:])

        step_through(0)
        step_emitted(0)
        step_through(1)
        step_first(0)
        step_emitted(1)
        step_second(0, whole)
        step_first(1)
        step_result(0, whole, nc.sync)
        for cols in halves:
            step_second(1, cols)
        for cols, queue in zip(halves, (nc.sync, nc.scalar)):
            step_result(1, cols, queue)
